import numpy as np
CORES = [16,32,48,64,80]
N = 5
TK = 256
NT = N * TK
EPS = 0.01
def setup_inputs(rng):
    x = (rng.standard_normal((N, 128, TK), dtype=np.float32) * (0.5 + np.arange(N, dtype=np.float32).reshape(N, 1, 1) / N) + rng.standard_normal((N, 128, 1), dtype=np.float32))
    return {"x": x, "dy": (rng.standard_normal((N, 128, TK), dtype=np.float32) + 0.5 * x + rng.standard_normal((1, 128, 1), dtype=np.float32))}
def reference(x, dy):
    X = x.astype(np.float64)
    mu = X.sum(axis=(0, 2)).reshape(1, 128, 1) / NT
    rs = 1.0 / np.sqrt(((X - mu) ** 2).sum(axis=(0, 2)).reshape(1, 128, 1) / NT + EPS)
    n = (X - mu) * rs
    DY = dy.astype(np.float64)
    a = DY.sum(axis=(0, 2)).reshape(1, 128, 1) / NT; c = (DY * n).sum(axis=(0, 2)).reshape(1, 128, 1) / NT
    return {"dx": (rs * (DY - a - n * c)).astype(np.float32)}

@@ -1,0 +1,125 @@
+import math
+
+from concourse.bass import DstId, RemoteDMATransfer
+from concourse.mybir import AluOpType, AxisListType, ActivationFunctionType
+
+EPS = 0.01
+W = 4
+
+SCRATCH = {
+    "xs": ("sbuf", [128, 256], "float32"),
+    "dys": ("sbuf", [128, 256], "float32"),
+    "prod": ("sbuf", [128, 256], "float32"),
+    "ja": ("sbuf", [128, 256], "float32"),
+    "jb": ("sbuf", [128, 256], "float32"),
+    "jc": ("sbuf", [128, 8], "float32"),
+    "w": ("sbuf", [128, 256], "float32"),
+    "dxs": ("sbuf", [128, 256], "float32"),
+    "land": ("sbuf", [128, 5 * W], "float32"),
+    "col": ("sbuf", [128, 12], "float32"),
+    "px": ("psum", [128, 512], "float32"),
+    "pt": ("psum", [128, 512], "float32"),
+}
+SEMAPHORES = ["ldx", "ldy", "cpx", "sx", "sxx", "sdy", "pr", "sxy", "arrived", "sent",
+              "gmu", "gxx", "t1", "sd", "ga", "gxy", "vv", "rv", "t2", "kn", "cn", "p1", "p2", "fin", "st"]
+
+
+def rank_program(g, core, T, topo):
+    rank = T.rank_of(core)
+    if rank is None:
+        return
+    n = len(T.cores)
+    tk = T.x.shape[1]
+    nt = n * tk
+    S = T.sem
+    V, A, Y = g.vector, g.scalar, g.sync
+    add, sub, mult = AluOpType.add, AluOpType.subtract, AluOpType.mult
+    Ident, Square, Sqrt = ActivationFunctionType.Identity, ActivationFunctionType.Square, ActivationFunctionType.Sqrt
+    X = AxisListType.X
+
+    o = rank * W
+    own = T.land[:, o:o + W]
+
+    def slot(j):
+        return T.land[:, o + j:o + j + 1]
+
+    def every(j):
+        return T.land[:, j:n * W:W]
+
+    def col(j):
+        return T.col[:, j:j + 1]
+
+    mu, exx, a, exy, t1, std, v, rv, t2, kn, cn = [col(j) for j in range(11)]
+
+    Y.dma_start(T.xs[:], T.x[:]).then_inc(S.ldx, 16)
+    A.dma_start(T.dys[:], T.dy[:]).then_inc(S.ldy, 16)
+
+    V.wait_ge(S.ldx, 16)
+    V.tensor_reduce(slot(0), T.xs[:], X, add).then_inc(S.sx, 1)
+    A.wait_ge(S.ldx, 16)
+    A.activation(T.px[:, 0:tk], T.xs[:], Ident, scale=1.0 / nt).then_inc(S.cpx, 1)
+    A.activation(T.ja[:], T.xs[:], Square, scale=1.0 / math.sqrt(nt), accum_out=slot(1)).then_inc(S.sxx, 1)
+    A.wait_ge(S.ldy, 16)
+    A.activation(T.jb[:], T.dys[:], Ident, scale=1.0 / nt, accum_out=slot(2)).then_inc(S.sdy, 1)
+    V.wait_ge(S.ldy, 16)
+    V.wait_ge(S.cpx, 1)
+    V.tensor_tensor(T.prod[:], T.dys[:], T.px[:, 0:tk], mult).then_inc(S.pr, 1)
+    V.wait_ge(S.pr, 1)
+    V.tensor_reduce(slot(3), T.prod[:], X, add).then_inc(S.sxy, 1)
+
+    others = [T.cores[(rank + d) % n] for d in range(1, n)]
+    mask = topo.mask(core, others[0])
+    for d in others:
+        assert topo.may_write(core, d) and topo.same_plane(topo.chip(core), topo.chip(d))
+        mask &= topo.mask(core, d)
+    engines = bin(mask).count("1")
+    ids = []
+    for d in others:
+        rid, pid, _se = topo.addr(d)
+        ids.append(DstId(rid=rid, pnc=pid))
+    for s in (S.sx, S.sxx, S.sdy, S.sxy):
+        g.wait_ge(s, 1)
+    g.remote_dma_fused([RemoteDMATransfer(dst_ids=ids, dma_engine_mask=mask, remote_sem=S.arrived,
+                                          srcs=[own], dsts=[own for _ in others], alu_op=0)], local_sem=S.sent)
+    landed = engines * len(others)
+
+    A.wait_ge(S.arrived, landed)
+    A.wait_ge(S.sx, 1)
+    A.activation(T.jc[:, 0:n], every(0), Ident, scale=1.0 / nt, accum_out=mu).then_inc(S.gmu, 1)
+    V.wait_ge(S.arrived, landed)
+    V.wait_ge(S.sxx, 1)
+    V.tensor_reduce(exx, every(1), X, add).then_inc(S.gxx, 1)
+    V.wait_ge(S.gxx, 1)
+    V.wait_ge(S.gmu, 1)
+    V.tensor_scalar(t1, mu, mu, exx, mult, sub).then_inc(S.t1, 1)
+    A.wait_ge(S.t1, 1)
+    A.activation(std, t1, Sqrt, bias=EPS, scale=-1.0).then_inc(S.sd, 1)
+
+    V.wait_ge(S.sdy, 1)
+    V.tensor_reduce(a, every(2), X, add).then_inc(S.ga, 1)
+    V.wait_ge(S.sxy, 1)
+    V.tensor_reduce(exy, every(3), X, add).then_inc(S.gxy, 1)
+    V.wait_ge(S.t1, 1)
+    V.tensor_scalar(v, t1, -1.0, EPS, mult, add).then_inc(S.vv, 1)
+    V.wait_ge(S.vv, 1)
+    V.reciprocal(rv, v).then_inc(S.rv, 1)
+    V.wait_ge(S.ga, 1)
+    V.wait_ge(S.gxy, 1)
+    V.tensor_scalar(t2, mu, a, exy, mult, sub).then_inc(S.t2, 1)
+    V.wait_ge(S.rv, 1)
+    V.wait_ge(S.t2, 1)
+    V.tensor_tensor(kn, t2, rv, mult).then_inc(S.kn, 1)
+    V.wait_ge(S.kn, 1)
+    V.tensor_scalar(cn, mu, kn, a, mult, add).then_inc(S.cn, 1)
+    V.wait_ge(S.cn, 1)
+    V.tensor_scalar(T.pt[:, 0:tk], T.xs[:], kn, cn, mult, sub).then_inc(S.p1, 1)
+    V.wait_ge(S.p1, 1)
+    V.tensor_tensor(T.w[:], T.dys[:], T.pt[:, 0:tk], add).then_inc(S.p2, 1)
+    V.wait_ge(S.p2, 1)
+    V.wait_ge(S.sd, 1)
+    V.tensor_scalar(T.dxs[:], T.w[:], rv, std, mult, mult).then_inc(S.fin, 1)
+
+    Y.wait_ge(S.fin, 1)
+    Y.dma_start(T.dx[:], T.dxs[:]).then_inc(S.st, 16)
+    Y.wait_ge(S.st, 16)
+    g.wait_ge(S.sent, engines)

@@ -5,6 +5,8 @@ from concourse.mybir import AluOpType, AxisListType, ActivationFunctionType
 
 EPS = 0.01
 W = 4
+U = 2
+CUTS = (0, 104, 192, 256)
 
 SCRATCH = {
     "xs": ("sbuf", [128, 256], "float32"),
@@ -13,15 +15,18 @@ SCRATCH = {
     "ja": ("sbuf", [128, 256], "float32"),
     "jb": ("sbuf", [128, 256], "float32"),
     "jc": ("sbuf", [128, 8], "float32"),
+    "xc": ("sbuf", [128, 256], "float32"),
     "w": ("sbuf", [128, 256], "float32"),
     "dxs": ("sbuf", [128, 256], "float32"),
-    "land": ("sbuf", [128, 5 * W], "float32"),
+    "lx": ("sbuf", [128, 5 * W], "float32"),
+    "ly": ("sbuf", [128, 5 * W], "float32"),
     "col": ("sbuf", [128, 12], "float32"),
     "px": ("psum", [128, 512], "float32"),
     "pt": ("psum", [128, 512], "float32"),
 }
-SEMAPHORES = ["ldx", "ldy", "cpx", "sx", "sxx", "sdy", "pr", "sxy", "arrived", "sent",
-              "gmu", "gxx", "t1", "sd", "ga", "gxy", "vv", "rv", "t2", "kn", "cn", "p1", "p2", "fin", "st"]
+SEMAPHORES = ["go", "ldx", "ldy", "cpx", "sx", "sxx", "sdy", "pr", "sxy", "arrx", "arry", "sent",
+              "gmu", "gxx", "t1", "sd", "ga", "gxy", "vv", "rv", "xc", "t2", "p1", "rs",
+              "w0", "w1", "w2", "f0", "f1", "f2", "st"]
 
 
 def rank_program(g, core, T, topo):
@@ -38,34 +43,16 @@ def rank_program(g, core, T, topo):
     X = AxisListType.X
 
     o = rank * W
-    own = T.land[:, o:o + W]
-
-    def slot(j):
-        return T.land[:, o + j:o + j + 1]
-
-    def every(j):
-        return T.land[:, j:n * W:W]
 
     def col(j):
         return T.col[:, j:j + 1]
 
-    mu, exx, a, exy, t1, std, v, rv, t2, kn, cn = [col(j) for j in range(11)]
+    mu, exx, a, exy, t1, std, v, rv, t2, rs = [col(j) for j in range(10)]
 
     Y.dma_start(T.xs[:], T.x[:]).then_inc(S.ldx, 16)
+    Y.sem_inc(S.go, 1)
+    A.wait_ge(S.go, 1)
     A.dma_start(T.dys[:], T.dy[:]).then_inc(S.ldy, 16)
-
-    V.wait_ge(S.ldx, 16)
-    V.tensor_reduce(slot(0), T.xs[:], X, add).then_inc(S.sx, 1)
-    A.wait_ge(S.ldx, 16)
-    A.activation(T.px[:, 0:tk], T.xs[:], Ident, scale=1.0 / nt).then_inc(S.cpx, 1)
-    A.activation(T.ja[:], T.xs[:], Square, scale=1.0 / math.sqrt(nt), accum_out=slot(1)).then_inc(S.sxx, 1)
-    A.wait_ge(S.ldy, 16)
-    A.activation(T.jb[:], T.dys[:], Ident, scale=1.0 / nt, accum_out=slot(2)).then_inc(S.sdy, 1)
-    V.wait_ge(S.ldy, 16)
-    V.wait_ge(S.cpx, 1)
-    V.tensor_tensor(T.prod[:], T.dys[:], T.px[:, 0:tk], mult).then_inc(S.pr, 1)
-    V.wait_ge(S.pr, 1)
-    V.tensor_reduce(slot(3), T.prod[:], X, add).then_inc(S.sxy, 1)
 
     others = [T.cores[(rank + d) % n] for d in range(1, n)]
     mask = topo.mask(core, others[0])
@@ -73,53 +60,88 @@ def rank_program(g, core, T, topo):
         assert topo.may_write(core, d) and topo.same_plane(topo.chip(core), topo.chip(d))
         mask &= topo.mask(core, d)
     engines = bin(mask).count("1")
+    landed = engines * len(others)
     ids = []
     for d in others:
         rid, pid, _se = topo.addr(d)
         ids.append(DstId(rid=rid, pnc=pid))
-    for s in (S.sx, S.sxx, S.sdy, S.sxy):
-        g.wait_ge(s, 1)
-    g.remote_dma_fused([RemoteDMATransfer(dst_ids=ids, dma_engine_mask=mask, remote_sem=S.arrived,
-                                          srcs=[own], dsts=[own for _ in others], alu_op=0)], local_sem=S.sent)
-    landed = engines * len(others)
 
-    A.wait_ge(S.arrived, landed)
+    def send(buf, sem):
+        own = buf[:, o:o + U]
+        g.remote_dma_fused([RemoteDMATransfer(dst_ids=ids, dma_engine_mask=mask, remote_sem=sem,
+                                              srcs=[own], dsts=[own for _ in others], alu_op=0)], local_sem=S.sent)
+
+    V.wait_ge(S.ldx, 16)
+    V.tensor_reduce(T.lx[:, o:o + 1], T.xs[:], X, add).then_inc(S.sx, 1)
+    A.wait_ge(S.ldx, 16)
+    A.activation(T.ja[:], T.xs[:], Square, scale=1.0 / math.sqrt(nt), accum_out=T.lx[:, o + 1:o + 2]).then_inc(S.sxx, 1)
+    g.wait_ge(S.sx, 1)
+    g.wait_ge(S.sxx, 1)
+    send(T.lx, S.arrx)
+
+    A.activation(T.px[:, 0:tk], T.xs[:], Ident, scale=1.0 / nt).then_inc(S.cpx, 1)
+    A.wait_ge(S.ldy, 16)
+    A.activation(T.jb[:], T.dys[:], Ident, scale=1.0 / nt, accum_out=T.ly[:, o:o + 1]).then_inc(S.sdy, 1)
+    V.wait_ge(S.ldy, 16)
+    V.wait_ge(S.cpx, 1)
+    V.tensor_tensor(T.prod[:], T.dys[:], T.px[:, 0:tk], mult).then_inc(S.pr, 1)
+    V.wait_ge(S.pr, 1)
+    V.tensor_reduce(T.ly[:, o + 1:o + 2], T.prod[:], X, add).then_inc(S.sxy, 1)
+    g.wait_ge(S.sdy, 1)
+    g.wait_ge(S.sxy, 1)
+    send(T.ly, S.arry)
+
+    A.wait_ge(S.arrx, landed)
     A.wait_ge(S.sx, 1)
-    A.activation(T.jc[:, 0:n], every(0), Ident, scale=1.0 / nt, accum_out=mu).then_inc(S.gmu, 1)
-    V.wait_ge(S.arrived, landed)
+    A.activation(T.jc[:, 0:n], T.lx[:, 0:n * W:W], Ident, scale=1.0 / nt, accum_out=mu).then_inc(S.gmu, 1)
+    V.wait_ge(S.arrx, landed)
     V.wait_ge(S.sxx, 1)
-    V.tensor_reduce(exx, every(1), X, add).then_inc(S.gxx, 1)
+    V.tensor_reduce(exx, T.lx[:, 1:n * W:W], X, add).then_inc(S.gxx, 1)
     V.wait_ge(S.gxx, 1)
     V.wait_ge(S.gmu, 1)
     V.tensor_scalar(t1, mu, mu, exx, mult, sub).then_inc(S.t1, 1)
     A.wait_ge(S.t1, 1)
     A.activation(std, t1, Sqrt, bias=EPS, scale=-1.0).then_inc(S.sd, 1)
 
-    V.wait_ge(S.sdy, 1)
-    V.tensor_reduce(a, every(2), X, add).then_inc(S.ga, 1)
-    V.wait_ge(S.sxy, 1)
-    V.tensor_reduce(exy, every(3), X, add).then_inc(S.gxy, 1)
     V.wait_ge(S.t1, 1)
     V.tensor_scalar(v, t1, -1.0, EPS, mult, add).then_inc(S.vv, 1)
     V.wait_ge(S.vv, 1)
     V.reciprocal(rv, v).then_inc(S.rv, 1)
+    V.wait_ge(S.rv, 1)
+    V.tensor_scalar(T.xc[:], T.xs[:], mu, rv, sub, mult).then_inc(S.xc, 1)
+    V.wait_ge(S.arry, landed)
+    V.wait_ge(S.sdy, 1)
+    V.tensor_reduce(a, T.ly[:, 0:n * W:W], X, add).then_inc(S.ga, 1)
+    V.wait_ge(S.sxy, 1)
+    V.tensor_reduce(exy, T.ly[:, 1:n * W:W], X, add).then_inc(S.gxy, 1)
     V.wait_ge(S.ga, 1)
     V.wait_ge(S.gxy, 1)
     V.tensor_scalar(t2, mu, a, exy, mult, sub).then_inc(S.t2, 1)
-    V.wait_ge(S.rv, 1)
     V.wait_ge(S.t2, 1)
-    V.tensor_tensor(kn, t2, rv, mult).then_inc(S.kn, 1)
-    V.wait_ge(S.kn, 1)
-    V.tensor_scalar(cn, mu, kn, a, mult, add).then_inc(S.cn, 1)
-    V.wait_ge(S.cn, 1)
-    V.tensor_scalar(T.pt[:, 0:tk], T.xs[:], kn, cn, mult, sub).then_inc(S.p1, 1)
+    V.wait_ge(S.xc, 1)
+    V.tensor_scalar(T.pt[:, 0:tk], T.xc[:], t2, a, mult, sub).then_inc(S.p1, 1)
     V.wait_ge(S.p1, 1)
-    V.tensor_tensor(T.w[:], T.dys[:], T.pt[:, 0:tk], add).then_inc(S.p2, 1)
-    V.wait_ge(S.p2, 1)
-    V.wait_ge(S.sd, 1)
-    V.tensor_scalar(T.dxs[:], T.w[:], rv, std, mult, mult).then_inc(S.fin, 1)
+    wsem = (S.w0, S.w1, S.w2)
+    fsem = (S.f0, S.f1, S.f2)
+    for b in range(3):
+        lo, hi = CUTS[b], CUTS[b + 1]
+        V.tensor_tensor(T.w[:, lo:hi], T.dys[:, lo:hi], T.pt[:, lo:hi], add).then_inc(wsem[b], 1)
 
-    Y.wait_ge(S.fin, 1)
+    A.wait_ge(S.sd, 1)
+    A.wait_ge(S.rv, 1)
+    A.activation(rs, std, Ident, scale=rv).then_inc(S.rs, 1)
+    A.wait_ge(S.rs, 1)
+    for b in range(2):
+        lo, hi = CUTS[b], CUTS[b + 1]
+        A.wait_ge(wsem[b], 1)
+        A.activation(T.dxs[:, lo:hi], T.w[:, lo:hi], Ident, scale=rs).then_inc(fsem[b], 1)
+    lo, hi = CUTS[2], CUTS[3]
+    V.wait_ge(wsem[2], 1)
+    V.wait_ge(S.sd, 1)
+    V.tensor_scalar(T.dxs[:, lo:hi], T.w[:, lo:hi], rv, std, mult, mult).then_inc(fsem[2], 1)
+
+    for s in fsem:
+        Y.wait_ge(s, 1)
     Y.dma_start(T.dx[:], T.dxs[:]).then_inc(S.st, 16)
     Y.wait_ge(S.st, 16)
-    g.wait_ge(S.sent, engines)
+    g.wait_ge(S.sent, 2 * engines)

import math

from concourse.bass import DstId, RemoteDMATransfer
from concourse.mybir import AluOpType, AxisListType, ActivationFunctionType

EPS = 0.01
W = 4
U = 2
CUTS = (0, 104, 192, 256)

SCRATCH = {
    "xs": ("sbuf", [128, 256], "float32"),
    "dys": ("sbuf", [128, 256], "float32"),
    "prod": ("sbuf", [128, 256], "float32"),
    "ja": ("sbuf", [128, 256], "float32"),
    "jb": ("sbuf", [128, 256], "float32"),
    "jc": ("sbuf", [128, 8], "float32"),
    "xc": ("sbuf", [128, 256], "float32"),
    "w": ("sbuf", [128, 256], "float32"),
    "dxs": ("sbuf", [128, 256], "float32"),
    "lx": ("sbuf", [128, 5 * W], "float32"),
    "ly": ("sbuf", [128, 5 * W], "float32"),
    "col": ("sbuf", [128, 12], "float32"),
    "px": ("psum", [128, 512], "float32"),
    "pt": ("psum", [128, 512], "float32"),
}
SEMAPHORES = ["go", "ldx", "ldy", "cpx", "sx", "sxx", "sdy", "pr", "sxy", "arrx", "arry", "sent",
              "gmu", "gxx", "t1", "sd", "ga", "gxy", "vv", "rv", "xc", "t2", "p1", "rs",
              "w0", "w1", "w2", "f0", "f1", "f2", "st"]


def rank_program(g, core, T, topo):
    rank = T.rank_of(core)
    if rank is None:
        return
    n = len(T.cores)
    tk = T.x.shape[1]
    nt = n * tk
    S = T.sem
    V, A, Y = g.vector, g.scalar, g.sync
    add, sub, mult = AluOpType.add, AluOpType.subtract, AluOpType.mult
    Ident, Square, Sqrt = ActivationFunctionType.Identity, ActivationFunctionType.Square, ActivationFunctionType.Sqrt
    X = AxisListType.X

    o = rank * W

    def col(j):
        return T.col[:, j:j + 1]

    mu, exx, a, exy, t1, std, v, rv, t2, rs = [col(j) for j in range(10)]

    Y.dma_start(T.xs[:], T.x[:]).then_inc(S.ldx, 16)
    Y.sem_inc(S.go, 1)
    A.wait_ge(S.go, 1)
    A.dma_start(T.dys[:], T.dy[:]).then_inc(S.ldy, 16)

    others = [T.cores[(rank + d) % n] for d in range(1, n)]
    mask = topo.mask(core, others[0])
    for d in others:
        assert topo.may_write(core, d) and topo.same_plane(topo.chip(core), topo.chip(d))
        mask &= topo.mask(core, d)
    engines = bin(mask).count("1")
    landed = engines * len(others)
    ids = []
    for d in others:
        rid, pid, _se = topo.addr(d)
        ids.append(DstId(rid=rid, pnc=pid))

    def send(buf, sem):
        own = buf[:, o:o + U]
        g.remote_dma_fused([RemoteDMATransfer(dst_ids=ids, dma_engine_mask=mask, remote_sem=sem,
                                              srcs=[own], dsts=[own for _ in others], alu_op=0)], local_sem=S.sent)

    V.wait_ge(S.ldx, 16)
    V.tensor_reduce(T.lx[:, o:o + 1], T.xs[:], X, add).then_inc(S.sx, 1)
    A.wait_ge(S.ldx, 16)
    A.activation(T.ja[:], T.xs[:], Square, scale=1.0 / math.sqrt(nt), accum_out=T.lx[:, o + 1:o + 2]).then_inc(S.sxx, 1)
    g.wait_ge(S.sx, 1)
    g.wait_ge(S.sxx, 1)
    send(T.lx, S.arrx)

    A.activation(T.px[:, 0:tk], T.xs[:], Ident, scale=1.0 / nt).then_inc(S.cpx, 1)
    A.wait_ge(S.ldy, 16)
    A.activation(T.jb[:], T.dys[:], Ident, scale=1.0 / nt, accum_out=T.ly[:, o:o + 1]).then_inc(S.sdy, 1)
    V.wait_ge(S.ldy, 16)
    V.wait_ge(S.cpx, 1)
    V.tensor_tensor(T.prod[:], T.dys[:], T.px[:, 0:tk], mult).then_inc(S.pr, 1)
    V.wait_ge(S.pr, 1)
    V.tensor_reduce(T.ly[:, o + 1:o + 2], T.prod[:], X, add).then_inc(S.sxy, 1)
    g.wait_ge(S.sdy, 1)
    g.wait_ge(S.sxy, 1)
    send(T.ly, S.arry)

    A.wait_ge(S.arrx, landed)
    A.wait_ge(S.sx, 1)
    A.activation(T.jc[:, 0:n], T.lx[:, 0:n * W:W], Ident, scale=1.0 / nt, accum_out=mu).then_inc(S.gmu, 1)
    V.wait_ge(S.arrx, landed)
    V.wait_ge(S.sxx, 1)
    V.tensor_reduce(exx, T.lx[:, 1:n * W:W], X, add).then_inc(S.gxx, 1)
    V.wait_ge(S.gxx, 1)
    V.wait_ge(S.gmu, 1)
    V.tensor_scalar(t1, mu, mu, exx, mult, sub).then_inc(S.t1, 1)
    A.wait_ge(S.t1, 1)
    A.activation(std, t1, Sqrt, bias=EPS, scale=-1.0).then_inc(S.sd, 1)

    V.wait_ge(S.t1, 1)
    V.tensor_scalar(v, t1, -1.0, EPS, mult, add).then_inc(S.vv, 1)
    V.wait_ge(S.vv, 1)
    V.reciprocal(rv, v).then_inc(S.rv, 1)
    V.wait_ge(S.rv, 1)
    V.tensor_scalar(T.xc[:], T.xs[:], mu, rv, sub, mult).then_inc(S.xc, 1)
    V.wait_ge(S.arry, landed)
    V.wait_ge(S.sdy, 1)
    V.tensor_reduce(a, T.ly[:, 0:n * W:W], X, add).then_inc(S.ga, 1)
    V.wait_ge(S.sxy, 1)
    V.tensor_reduce(exy, T.ly[:, 1:n * W:W], X, add).then_inc(S.gxy, 1)
    V.wait_ge(S.ga, 1)
    V.wait_ge(S.gxy, 1)
    V.tensor_scalar(t2, mu, a, exy, mult, sub).then_inc(S.t2, 1)
    V.wait_ge(S.t2, 1)
    V.wait_ge(S.xc, 1)
    V.tensor_scalar(T.pt[:, 0:tk], T.xc[:], t2, a, mult, sub).then_inc(S.p1, 1)
    V.wait_ge(S.p1, 1)
    wsem = (S.w0, S.w1, S.w2)
    fsem = (S.f0, S.f1, S.f2)
    for b in range(3):
        lo, hi = CUTS[b], CUTS[b + 1]
        V.tensor_tensor(T.w[:, lo:hi], T.dys[:, lo:hi], T.pt[:, lo:hi], add).then_inc(wsem[b], 1)

    A.wait_ge(S.sd, 1)
    A.wait_ge(S.rv, 1)
    A.activation(rs, std, Ident, scale=rv).then_inc(S.rs, 1)
    A.wait_ge(S.rs, 1)
    for b in range(2):
        lo, hi = CUTS[b], CUTS[b + 1]
        A.wait_ge(wsem[b], 1)
        A.activation(T.dxs[:, lo:hi], T.w[:, lo:hi], Ident, scale=rs).then_inc(fsem[b], 1)
    lo, hi = CUTS[2], CUTS[3]
    V.wait_ge(wsem[2], 1)
    V.wait_ge(S.sd, 1)
    V.tensor_scalar(T.dxs[:, lo:hi], T.w[:, lo:hi], rv, std, mult, mult).then_inc(fsem[2], 1)

    for s in fsem:
        Y.wait_ge(s, 1)
    Y.dma_start(T.dx[:], T.dxs[:]).then_inc(S.st, 16)
    Y.wait_ge(S.st, 16)
    g.wait_ge(S.sent, 2 * engines)
